import numpy as np, ml_dtypes
CORES = [83,85,87,115,117,119]
N = 6
BF = ml_dtypes.bfloat16
def gentries(a):
    return np.ascontiguousarray(a.reshape(8, 16, -1).transpose(0, 2, 1)).reshape(8, -1)
def gtable(e):
    e = np.asarray(e); return np.ascontiguousarray(e.reshape(8, -1, 16).transpose(0, 2, 1)).reshape(128, -1).astype(np.int32)
K, D, SH = 1024, 2048, 5
def sized(rng):
    return rng.standard_normal((N, 128, D), dtype=np.float32) * np.exp2(rng.integers(-1, 2, (N, 128, 1))).astype(np.float32)
def hashes(a, b):
    return np.repeat(np.stack([a, b], 2), 16, axis=1).astype(np.int32)
def lists(e):
    return np.stack([gtable(u) for u in e])
def setup_inputs(rng):
    a = np.stack([rng.permutation(255)[:8] + 1 for r in range(N)]); b = rng.integers(0, 65536, (N, 8))
    return {"mat": sized(rng).astype(BF), "ids": lists(rng.integers(0, 65536, (N, 8, K))), "hs": hashes(a, b)}
def setup_inputs_ends(rng):
    e = rng.integers(0, 65536, (N, 8, K)); e = np.where(rng.random(e.shape) < 0.5, rng.choice(np.array([0, 1, 65534, 65535]), e.shape), e)
    e[:, :, 0] = 0; e[:, :, 1] = 1 << SH; e[:, :, -1] = 65535
    top = (D - 1) << SH; low = (1 << SH) - 1
    a = rng.choice(np.array([0, 1, 254, 255]), (N, 8)); b = rng.choice(np.array([0, 1, low, top, top + low, 65535]), (N, 8))
    for r in range(N):
        a[r, r % 8], b[r, r % 8] = 1, top
        a[r, (r + 1) % 8], b[r, (r + 1) % 8] = 255, 65535
        a[r, (r + 2) % 8] = 0
        a[r, (r + 3) % 8], b[r, (r + 3) % 8] = 1, top + low
    return {"mat": sized(rng).astype(BF), "ids": lists(e), "hs": hashes(a, b)}
def setup_inputs_one(rng):
    d = setup_inputs(rng); e = rng.integers(0, 65536, (N, 8, K)); o = rng.permutation(N)
    e[o[0]] = rng.permutation(65536)[:8, None]; e[o[1]] = e[o[2]]; e[o[3]] = np.repeat(e[o[3], :, :K // 16], 16, axis=1)
    d["ids"] = lists(e); d["hs"][rng.integers(0, N), :, 0] = 0; return d
def setup_inputs_turns(rng):
    d = setup_inputs(rng); p = np.argsort(rng.random((N, 8, D, 4)), axis=3)
    w = (rng.integers(128, 256, p.shape) * (2 * rng.integers(0, 2, p.shape) - 1)).astype(np.float32) * np.float32(2.0 ** -7)
    m = np.where(p[..., None] == np.arange(4), w[..., None], np.float32(0))
    d["mat"] = np.ascontiguousarray(m.transpose(0, 1, 3, 4, 2)).reshape(N, 128, D).astype(BF); return d
def setup_inputs_spread(rng):
    d = setup_inputs(rng); k = (N, 8, 1, D)
    z = (np.exp2(rng.integers(-2, 3, k)) * (rng.random(k) > 0.03125)).astype(np.float32)
    d["mat"] = (sized(rng).reshape(N, 8, 16, D) * z).reshape(N, 128, D).astype(BF); return d
def check_inputs(d):
    bad = []; h = d["hs"].reshape(N, 8, 16, 2)
    if not (np.abs(d["mat"].astype(np.float32)) <= 8192).all(): bad.append("size of mat")
    if not ((d["ids"] >= 0) & (d["ids"] <= 65535)).all(): bad.append("range of ids")
    if not ((h >= 0) & (h <= np.array([255, 65535]))).all(): bad.append("range of hs")
    if not (h == h[:, :, :1]).all(): bad.append("rows of hs alike in a group")
    return bad
def reference(mat, ids, hs):
    y = np.zeros((N, 32, K), np.float64); m = mat.astype(np.float64).reshape(N, 8, 16, D); h = hs.astype(np.int64)[:, ::16]
    for r in range(N):
        i = gentries(ids[r]).astype(np.int64)
        v = np.zeros((8, 4, K), np.float64); v[:, 0] = 1
        for q in range(N):
            t = ((i * h[q, :, :1] + h[q, :, 1:]) >> SH) & (D - 1)
            x = np.take_along_axis(m[q], t[:, None, :], 2).reshape(8, 4, 4, K)
            v = np.sum(v[:, :, None, :] * x, axis=1)
        y[r] = v.reshape(32, K)
    return {"y": y.astype(np.float32)}

@@ -1,0 +1,247 @@
+from concourse.bass import DstId, RemoteDMATransfer
+from concourse.mybir import AluOpType, ActivationFunctionType
+
+N, D, K = 6, 2048, 1024
+NR = 4
+QW = D // NR
+NB = 2
+BW = K // NB
+
+SCRATCH = {
+    "idt": ("sbuf", [128, K // 16], "int32"),
+    "hsall": ("dram", [N, 128, 2], "int32"),
+    "hrow": ("sbuf", [128, 256], "int32"),
+    "hta": ("sbuf", [128, 128], "float32"),
+    "htb": ("sbuf", [128, 128], "float32"),
+    "xi": ("sbuf", [128, N * K // 16], "int32"),
+    "xj": ("sbuf", [128, N * K // 16], "int32"),
+    "off": ("sbuf", [128, N * K // 16], "uint16"),
+    "pi": ("sbuf", [128, 8], "int32"),
+    "pg": ("sbuf", [128, 8], "int32"),
+    "pc": ("sbuf", [128, 8], "int32"),
+    "pa": ("sbuf", [128, 8], "int32"),
+    "pf": ("sbuf", [128, 8], "float32"),
+    "key": ("sbuf", [128, 8], "float32"),
+    "pa2": ("sbuf", [128, 8], "float32"),
+    "key0": ("sbuf", [128, 8], "float32"),
+    "mq": ("sbuf", [128, 128], "float32"),
+    "my": ("sbuf", [128, 32], "float32"),
+    "wm": ("sbuf", [128, 128], "float32"),
+    "wy": ("sbuf", [128, 32], "float32"),
+    "ws": ("sbuf", [128, 128], "bfloat16"),
+    "eye": ("sbuf", [128, 8], "float32"),
+    "ysb": ("sbuf", [128, K], "float32"),
+    "psh": ("psum", [128, 512], "float32"),
+}
+for _q in range(N):
+    SCRATCH["win%d" % _q] = ("sbuf", [128, D], "bfloat16")
+    SCRATCH["gat%d" % _q] = ("sbuf", [128, K], "bfloat16")
+    SCRATCH["rl%d" % _q] = ("sbuf", [128, QW], "bfloat16")
+for _b in range(NB):
+    SCRATCH["prod%d" % _b] = ("sbuf", [128, BW], "float32")
+    SCRATCH["v%d" % _b] = ("psum", [128, 512], "float32")
+
+SEMAPHORES = ["hsl", "idl", "matl", "hsarr", "hl", "sent", "iot", "cst", "hcv", "hps", "lst", "stored", "yc"]
+SEMAPHORES += ["tab%d" % q for q in range(N)] + ["ra%d" % q for q in range(N)]
+SEMAPHORES += ["gs%d_%d" % (q, b) for q in range(N) for b in range(NB)]
+SEMAPHORES += ["pe%d" % b for b in range(NB)] + ["dv%d" % b for b in range(NB)]
+
+
+def relays(cores, q, topo):
+    far = [c for c in cores if topo.chip(c) != topo.chip(cores[q])]
+    idle = [c for c in topo.cores_of(far[0]) if c not in cores]
+    d0 = [c for c in idle if topo.die(c) == 0]
+    d1 = [c for c in idle if topo.die(c) == 1]
+    return (d0[:NR // 2] + d1[:NR // 2]), far
+
+
+def dst(topo, c):
+    a = topo.addr(c)
+    return DstId(rid=a[0], pnc=a[1])
+
+
+def bits(engines):
+    m = 0
+    for e in engines:
+        m |= 1 << e
+    return m
+
+
+def relay_program(g, core, T, topo):
+    n = 0
+    for q in range(N):
+        rel, far = relays(T.cores, q, topo)
+        if core not in rel:
+            continue
+        k = rel.index(core)
+        g.wait_ge(T.sem["ra%d" % q], 2)
+        win = T["win%d" % q]
+        m = topo.mask(core, far[0])
+        g.remote_dma_fused([RemoteDMATransfer(
+            dst_ids=[dst(topo, c) for c in far], dma_engine_mask=m, remote_sem=T.sem["tab%d" % q],
+            srcs=[T["rl%d" % q][:, :]], dsts=[win[:, k * QW:(k + 1) * QW] for c in far])], local_sem=T.sem.sent)
+        n += len(topo.engines(core, far[0]))
+    if n:
+        g.wait_ge(T.sem.sent, n)
+
+
+def rank_program(g, core, T, topo):
+    rank = T.rank_of(core)
+    cores = list(T.cores)
+    if rank is None:
+        relay_program(g, core, T, topo)
+        return
+    r = rank
+    A = AluOpType
+    S = T.sem
+    near = [c for c in cores if c != core and topo.chip(c) == topo.chip(core)]
+    rel, far = relays(cores, r, topo)
+    e_off = topo.engines(core, far[0])
+    e_on = [e for e in topo.engines(core, near[0]) if e not in e_off]
+    own = T["win%d" % r]
+
+    g.sync.dma_start(T.hsall[r], T.hs[:, :]).then_inc(S.hsl, 16)
+    g.scalar.dma_start(own[:, :], T.mat[:, :]).then_inc(S.matl, 16)
+    g.sync.dma_start(T.idt[:, :], T.ids[:, :]).then_inc(S.idl, 16)
+
+    g.iota(T.pi[:, 0:1], [[0, 1]], 0, 1).then_inc(S.iot, 1)
+    g.iota(T.mq[:, :], [[1, 32], [0, 4]], 0, 0, allow_small_or_imprecise_dtypes=True).then_inc(S.iot, 1)
+    g.iota(T.my[:, :], [[1, 32]], 0, 0, allow_small_or_imprecise_dtypes=True).then_inc(S.iot, 1)
+    g.wait_ge(S.hsl, 16)
+    g.remote_dma_fused([
+        RemoteDMATransfer(dst_ids=[dst(topo, c) for c in far], dma_engine_mask=bits(e_off), remote_sem=S.hsarr,
+                          srcs=[T.hsall[r]], dsts=[T.hsall[r] for c in far]),
+        RemoteDMATransfer(dst_ids=[dst(topo, c) for c in near], dma_engine_mask=bits(e_on), remote_sem=S.hsarr,
+                          srcs=[T.hsall[r]], dsts=[T.hsall[r] for c in near])], local_sem=S.sent)
+    g.wait_ge(S.matl, 16)
+
+    def send_off():
+        g.remote_dma_fused([RemoteDMATransfer(
+            dst_ids=[dst(topo, rel[k])], dma_engine_mask=bits(e_off[2 * k:2 * k + 2]), remote_sem=S["ra%d" % r],
+            srcs=[own[:, k * QW:(k + 1) * QW]], dsts=[T["rl%d" % r][:, :]]) for k in range(NR)], local_sem=S.sent)
+
+    def send_on():
+        g.remote_dma_fused([RemoteDMATransfer(
+            dst_ids=[dst(topo, c) for c in near], dma_engine_mask=bits(e_on), remote_sem=S["tab%d" % r],
+            srcs=[own[:, :]], dsts=[own[:, :] for c in near])], local_sem=S.sent)
+
+    if r == 2:
+        send_on()
+        send_off()
+    else:
+        send_off()
+        send_on()
+    g.wait_ge(S.sent, 2 * (len(e_off) + len(e_on)))
+
+    g.sync.wait_ge(S.hsl, 16)
+    g.sync.wait_ge(S.hsarr, len(e_off) * len(far) + len(e_on) * len(near))
+    g.sync.dma_start(T.hrow[0:N, :], T.hsall[:, :, :]).then_inc(S.hl, 16)
+
+    v = g.vector
+    nc = [0]
+
+    def c(ins):
+        nc[0] += 1
+        ins.then_inc(S.cst, 1)
+
+    v.wait_ge(S.iot, 3)
+    c(v.tensor_scalar(T.pg[:, 0:1], T.pi[:, 0:1], 2, 28, A.logical_shift_right, A.bitwise_and))
+    c(v.tensor_scalar(T.pc[:, 0:1], T.pi[:, 0:1], 3, None, A.bitwise_and))
+    c(v.tensor_scalar(T.pa[:, 0:1], T.pi[:, 0:1], 2, 3, A.logical_shift_right, A.bitwise_and))
+    c(v.tensor_copy(T.pf[:, 0:1], T.pi[:, 0:1]))
+    v.wait_ge(S.cst, nc[0])
+    c(v.tensor_tensor(T.key[:, 0:1], T.pg[:, 0:1], T.pc[:, 0:1], A.add))
+    c(v.tensor_scalar(T.pa2[:, 0:1], T.pa[:, 0:1], 100.0, None, A.mult))
+    c(v.tensor_scalar(T.eye[0:N, 0:N], T.my[0:N, 0:N], T.pf[0:N, 0:1], None, A.is_equal))
+    v.wait_ge(S.cst, nc[0])
+    c(v.tensor_tensor(T.key0[:, 0:1], T.key[:, 0:1], T.pa2[:, 0:1], A.add))
+    c(v.tensor_scalar(T.wm[:, :], T.mq[:, :], T.key[:, 0:1], None, A.is_equal))
+    c(v.tensor_scalar(T.wy[:, :], T.my[:, :], T.key[:, 0:1], None, A.is_equal))
+    v.wait_ge(S.cst, nc[0])
+    c(v.tensor_scalar(T.ws[:, :], T.mq[:, :], T.key0[:, 0:1], None, A.is_equal))
+    ncst = nc[0]
+
+    v.wait_ge(S.hl, 16)
+    v.tensor_copy(T.hta[0:N, :], T.hrow[0:N, 0::2]).then_inc(S.hcv, 1)
+    v.tensor_copy(T.htb[0:N, :], T.hrow[0:N, 1::2]).then_inc(S.hcv, 1)
+    g.tensor.wait_ge(S.cst, ncst)
+    g.tensor.wait_ge(S.hcv, 2)
+    g.tensor.matmul(T.psh[:, 0:N], T.hta[0:N, :], T.eye[0:N, 0:N], True, True).then_inc(S.hps, 1)
+    g.tensor.matmul(T.psh[:, 8:8 + N], T.htb[0:N, :], T.eye[0:N, 0:N], True, True).then_inc(S.hps, 1)
+    v.wait_ge(S.idl, 16)
+    v.wait_ge(S.hps, 2)
+    L = K // 16
+    for q in range(N):
+        v.tensor_scalar(T.xi[:, q * L:(q + 1) * L], T.idt[:, :], T.psh[:, q:q + 1], T.psh[:, 8 + q:9 + q],
+                        A.mult, A.add).then_inc(S.lst, 1)
+    v.wait_ge(S.lst, N)
+    v.tensor_scalar(T.xj[:, :], T.xi[:, :], 5, D - 1, A.logical_shift_right, A.bitwise_and).then_inc(S.lst, 1)
+    v.wait_ge(S.lst, N + 1)
+    v.tensor_copy(T.off[:, :], T.xj[:, :]).then_inc(S.lst, 1)
+
+    arrive = {}
+    for q in range(N):
+        if q == r:
+            arrive[q] = (S.matl, 16)
+        elif cores[q] in near:
+            arrive[q] = (S["tab%d" % q], len(e_on))
+        else:
+            arrive[q] = (S["tab%d" % q], NR * len(topo.engines(rel[0], far[0])))
+    LB = BW // 16
+
+    def pick(eng, q, b):
+        eng.wait_ge(*arrive[q])
+        o = T["gat%d" % q][:, b * BW:(b + 1) * BW]
+        i = T["win%d" % q][:, :].indirect(T.off[:, q * L + b * LB:q * L + (b + 1) * LB])
+        if eng is g.scalar:
+            eng.activation(o, i, ActivationFunctionType.Copy).then_inc(S["gs%d_%d" % (q, b)], 1)
+        else:
+            eng.tensor_copy(o, i).then_inc(S["gs%d_%d" % (q, b)], 1)
+
+    onchip = [q for q in range(N) if cores[q] in near]
+    if r in (0, 1, 2):
+        order = [r] + [q for q in range(N) if q != r and not (q == 1)]
+        vq = 1 if r != 1 else None
+    else:
+        order = [r, onchip[0], 0, 2] + [onchip[1]]
+        vq = 1
+    g.scalar.wait_ge(S.lst, N + 2)
+    for q in order:
+        for b in range(NB):
+            pick(g.scalar, q, b)
+
+    t = g.tensor
+    for b in range(NB):
+        t.wait_ge(S["gs0_%d" % b], 1)
+        t.matmul(T["v%d" % b][:, 0:BW], T.ws[:, :], T.gat0[:, b * BW:(b + 1) * BW], True, True).then_inc(S["pe%d" % b], 1)
+    for q in range(1, N):
+        for b in range(NB):
+            t.wait_ge(S["dv%d" % b], q)
+            if q < N - 1:
+                t.matmul(T["v%d" % b][:, 0:BW], T.wm[:, :], T["prod%d" % b][:, :], True, True).then_inc(S["pe%d" % b], 1)
+            else:
+                t.matmul(T["v%d" % b][0:32, 0:BW], T.wy[:, :], T["prod%d" % b][:, :], True, True).then_inc(S["pe%d" % b], 1)
+    v.wait_ge(S.lst, N + 2)
+    for q in range(1, N):
+        for b in range(NB):
+            if q == vq:
+                pick(v, q, b)
+            v.wait_ge(S["gs%d_%d" % (q, b)], 1)
+            v.wait_ge(S["pe%d" % b], q)
+            v.tensor_tensor(T["prod%d" % b][:, :], T["v%d" % b][:, 0:BW], T["gat%d" % q][:, b * BW:(b + 1) * BW],
+                            A.mult).then_inc(S["dv%d" % b], 1)
+
+    for b in range(NB):
+        cols = slice(b * BW, (b + 1) * BW)
+        e = g.scalar if b % 2 == 0 else v
+        e.wait_ge(S["pe%d" % b], N)
+        if b % 2 == 0:
+            e.activation(T.ysb[0:32, cols], T["v%d" % b][0:32, 0:BW], ActivationFunctionType.Copy).then_inc(S.yc, 1)
+        else:
+            e.tensor_copy(T.ysb[0:32, cols], T["v%d" % b][0:32, 0:BW]).then_inc(S.stored, 1)
+    g.scalar.wait_ge(S.yc, 1)
+    g.scalar.dma_start(T.y[:, 0:BW], T.ysb[0:32, 0:BW]).then_inc(S.yc, 16)
+    g.sync.wait_ge(S.stored, 1)
+    g.sync.dma_start(T.y[:, BW:K], T.ysb[0:32, BW:K]).then_inc(S.stored, 16)
+    g.scalar.wait_ge(S.yc, 17)
+    g.sync.wait_ge(S.stored, 17)

@@ -4,55 +4,125 @@ from concourse.mybir import AluOpType, ActivationFunctionType
 N, D, K = 6, 2048, 1024
 NR = 4
 QW = D // NR
-NB = 2
+H = D // 2
+NB = 4
 BW = K // NB
+L = K // 16
+LB = BW // 16
+FORWARD = {1: [0], 2: [0, 1], 5: [0, 1]}
 
 SCRATCH = {
-    "idt": ("sbuf", [128, K // 16], "int32"),
-    "hsall": ("dram", [N, 128, 2], "int32"),
-    "hrow": ("sbuf", [128, 256], "int32"),
-    "hta": ("sbuf", [128, 128], "float32"),
-    "htb": ("sbuf", [128, 128], "float32"),
-    "xi": ("sbuf", [128, N * K // 16], "int32"),
-    "xj": ("sbuf", [128, N * K // 16], "int32"),
-    "off": ("sbuf", [128, N * K // 16], "uint16"),
+    "idt": ("sbuf", [128, L], "int32"),
+    "hd": ("dram", [128, 2], "int32"),
+    "hfar": ("dram", [128, 2], "int32"),
+    "hnear": ("dram", [128, 2], "int32"),
+    "t0": ("dram", [NR, 128, 128], "bfloat16"),
+    "hx": ("sbuf", [128, 2 * N], "int32"),
+    "hf": ("sbuf", [128, 2 * N], "float32"),
+    "xi": ("sbuf", [128, N * L], "int32"),
+    "xj": ("sbuf", [128, N * L], "int32"),
+    "off": ("sbuf", [128, N * L], "uint16"),
     "pi": ("sbuf", [128, 8], "int32"),
     "pg": ("sbuf", [128, 8], "int32"),
     "pc": ("sbuf", [128, 8], "int32"),
-    "pa": ("sbuf", [128, 8], "int32"),
-    "pf": ("sbuf", [128, 8], "float32"),
     "key": ("sbuf", [128, 8], "float32"),
-    "pa2": ("sbuf", [128, 8], "float32"),
-    "key0": ("sbuf", [128, 8], "float32"),
     "mq": ("sbuf", [128, 128], "float32"),
     "my": ("sbuf", [128, 32], "float32"),
     "wm": ("sbuf", [128, 128], "float32"),
     "wy": ("sbuf", [128, 32], "float32"),
-    "ws": ("sbuf", [128, 128], "bfloat16"),
-    "eye": ("sbuf", [128, 8], "float32"),
     "ysb": ("sbuf", [128, K], "float32"),
-    "psh": ("psum", [128, 512], "float32"),
 }
 for _q in range(N):
     SCRATCH["win%d" % _q] = ("sbuf", [128, D], "bfloat16")
-    SCRATCH["gat%d" % _q] = ("sbuf", [128, K], "bfloat16")
     SCRATCH["rl%d" % _q] = ("sbuf", [128, QW], "bfloat16")
+    if _q != 1:
+        SCRATCH["gat%d" % _q] = ("sbuf", [128, K], "bfloat16")
 for _b in range(NB):
     SCRATCH["prod%d" % _b] = ("sbuf", [128, BW], "float32")
     SCRATCH["v%d" % _b] = ("psum", [128, 512], "float32")
 
-SEMAPHORES = ["hsl", "idl", "matl", "hsarr", "hl", "sent", "iot", "cst", "hcv", "hps", "lst", "stored", "yc"]
-SEMAPHORES += ["tab%d" % q for q in range(N)] + ["ra%d" % q for q in range(N)]
+SEMAPHORES = ["hsl", "hxl", "idl", "mata", "matb", "pk", "w0", "ha", "hb", "hsarr", "sent", "iot", "cst", "hcv", "lst"]
+SEMAPHORES += ["%s%d" % (s, q) for q in range(N) for s in ("tab", "fst", "ra")]
 SEMAPHORES += ["gs%d_%d" % (q, b) for q in range(N) for b in range(NB)]
-SEMAPHORES += ["pe%d" % b for b in range(NB)] + ["dv%d" % b for b in range(NB)]
+SEMAPHORES += ["%s%d" % (s, b) for b in range(NB) for s in ("pe", "dv", "yc")]
 
 
-def relays(cores, q, topo):
-    far = [c for c in cores if topo.chip(c) != topo.chip(cores[q])]
-    idle = [c for c in topo.cores_of(far[0]) if c not in cores]
-    d0 = [c for c in idle if topo.die(c) == 0]
-    d1 = [c for c in idle if topo.die(c) == 1]
-    return (d0[:NR // 2] + d1[:NR // 2]), far
+def sides(cores, q, topo):
+    me = cores[q]
+    near = [c for c in cores if c != me and topo.chip(c) == topo.chip(me)]
+    far = [c for c in cores if topo.chip(c) != topo.chip(me)]
+    e_off = topo.engines(me, far[0])
+    e_all = topo.engines(me, near[0])
+    return near, far, helpers(cores, far[0], topo), e_off, [e for e in e_all if e not in e_off], e_all
+
+
+def helpers(cores, c, topo):
+    idle = [x for x in topo.cores_of(c) if x not in cores]
+    return [x for x in idle if topo.die(x) == 1][:NR // 2] + [x for x in idle if topo.die(x) == 0][:NR // 2]
+
+
+def cols(k):
+    return (k * QW, (k + 1) * QW)
+
+
+def plan(cores, q, topo):
+    near, far, rel, e_off, e_on, e_all = sides(cores, q, topo)
+    tab, fst, ra, win, rl = ["%s%d" % (s, q) for s in ("tab", "fst", "ra", "win", "rl")]
+
+    def rp(k, es):
+        return ([rel[k]], es, ra, cols(k), rl)
+
+    if q == 0:
+        return ["pk", [([rel[k]], e_off[2 * k:2 * k + 2], ra, k, "t0") for k in range(NR)],
+                "w0", [(near, e_on, tab, (0, H), win)], [(near, e_all, tab, (H, D), win)]]
+    if q == 1:
+        f = forwarder(cores, q, topo)
+        o = [c for c in near if c != f]
+        return ["mata", [rp(1, e_off), ([f], e_on, fst, cols(0), win)],
+                "matb", [rp(2, e_off[:4]), rp(3, e_off[4:]), (near, e_on, tab, cols(1), win)],
+                [(o, e_on, tab, cols(0), win)],
+                [(near, e_all, tab, (H, D), win)]]
+    if q in FORWARD:
+        return ["mata", [(near, e_all, fst, (0, H), win)],
+                "matb", [(near, e_all, tab, (H, D), win)],
+                [rp(2, e_off[:4]), rp(3, e_off[4:])]]
+    return ["mata", [rp(0, e_off[:4]), rp(1, e_off[4:])],
+            [(near, e_on, tab, (0, H), win)],
+            "matb", [rp(2, e_off[:4]), rp(3, e_off[4:])],
+            [(near, e_all, tab, (H, D), win)]]
+
+
+def forwarder(cores, q, topo):
+    return [c for c in cores if topo.chip(c) == topo.chip(cores[q]) and topo.die(c) != topo.die(cores[q])][0]
+
+
+def forwards(cores, q, topo):
+    rel = sides(cores, q, topo)[2]
+    es = topo.engines(forwarder(cores, q, topo), rel[0])
+    w = len(es) // len(FORWARD[q])
+    return [([rel[k]], es[w * i:w * i + w], "ra%d" % q, cols(k), "rl%d" % q) for i, k in enumerate(FORWARD[q])]
+
+
+def hand_on(cores, q, k, topo):
+    near, far, rel, e_off, e_on, e_all = sides(cores, q, topo)
+    return [(far, topo.engines(rel[k], far[0]), "tab%d" % q, cols(k), "win%d" % q)]
+
+
+def hash_cores(cores, q, topo):
+    near, far = sides(cores, q, topo)[:2]
+    i = sorted(near + [cores[q]]).index(cores[q])
+    return helpers(cores, far[0], topo)[i], helpers(cores, cores[q], topo)[i + 1]
+
+
+def count(cores, topo, sem, core):
+    n = 0
+    for q in range(N):
+        calls = [x for x in plan(cores, q, topo) if isinstance(x, list)]
+        calls += [forwards(cores, q, topo)] if q in FORWARD else []
+        calls += [hand_on(cores, q, k, topo) for k in range(NR)]
+        for call in calls:
+            n += sum(len(x[1]) for x in call if x[2] == sem and core in x[0])
+    return n
 
 
 def dst(topo, c):
@@ -67,77 +137,100 @@ def bits(engines):
     return m
 
 
+def part(T, buf, where):
+    if buf == "t0":
+        return T.t0[where]
+    if buf[:2] == "rl" or buf in ("hd", "hfar", "hnear"):
+        return T[buf][:, :]
+    return T[buf][:, where[0]:where[1]]
+
+
+def send(g, T, topo, call, src):
+    g.remote_dma_fused([RemoteDMATransfer(
+        dst_ids=[dst(topo, c) for c in to], dma_engine_mask=bits(es), remote_sem=T.sem[sem],
+        srcs=[part(T, src, where)], dsts=[part(T, buf, where) for c in to])
+        for to, es, sem, where, buf in call], local_sem=T.sem.sent)
+    return sum(len(x[1]) for x in call)
+
+
+def spread(T, table, win, queues, sem):
+    for c in range(4):
+        for i in range(4):
+            queues[i % 2].dma_start(win[4 * c + i::16, :], table(c)).then_inc(sem, 16)
+
+
 def relay_program(g, core, T, topo):
+    cores = list(T.cores)
+    S = T.sem
+    if core not in helpers(cores, core, topo):
+        return
     n = 0
+    for near in (True, False):
+        for q in range(N):
+            if core == hash_cores(cores, q, topo)[1 if near else 0]:
+                to = [c for c in cores if topo.chip(c) == topo.chip(core) and c != cores[q]]
+                es = topo.engines(core, to[0])
+                qr = sides(cores, q, topo)
+                g.wait_ge(S.hb if near else S.ha, len(qr[4] if near else qr[3]))
+                n += send(g, T, topo, [(to, es, "hsarr", (2 * q, 2 * q + 2), "hx")], "hnear" if near else "hfar")
     for q in range(N):
-        rel, far = relays(T.cores, q, topo)
-        if core not in rel:
-            continue
-        k = rel.index(core)
-        g.wait_ge(T.sem["ra%d" % q], 2)
-        win = T["win%d" % q]
-        m = topo.mask(core, far[0])
-        g.remote_dma_fused([RemoteDMATransfer(
-            dst_ids=[dst(topo, c) for c in far], dma_engine_mask=m, remote_sem=T.sem["tab%d" % q],
-            srcs=[T["rl%d" % q][:, :]], dsts=[win[:, k * QW:(k + 1) * QW] for c in far])], local_sem=T.sem.sent)
-        n += len(topo.engines(core, far[0]))
-    if n:
-        g.wait_ge(T.sem.sent, n)
+        rel = sides(cores, q, topo)[2]
+        if core in rel:
+            k = rel.index(core)
+            if q == 0:
+                for e in (g.sync, g.scalar):
+                    e.wait_ge(S.ra0, count(cores, topo, "ra0", core))
+                spread(T, lambda c: T.t0[k, 32 * c:32 * c + 32, :], T.rl0, (g.sync, g.scalar), S.w0)
+                g.wait_ge(S.w0, 256)
+            else:
+                g.wait_ge(S["ra%d" % q], count(cores, topo, "ra%d" % q, core))
+            n += send(g, T, topo, hand_on(cores, q, k, topo), "rl%d" % q)
+    g.wait_ge(S.sent, n)
 
 
 def rank_program(g, core, T, topo):
-    rank = T.rank_of(core)
+    r = T.rank_of(core)
     cores = list(T.cores)
-    if rank is None:
+    if r is None:
         relay_program(g, core, T, topo)
         return
-    r = rank
     A = AluOpType
     S = T.sem
-    near = [c for c in cores if c != core and topo.chip(c) == topo.chip(core)]
-    rel, far = relays(cores, r, topo)
-    e_off = topo.engines(core, far[0])
-    e_on = [e for e in topo.engines(core, near[0]) if e not in e_off]
+    v = g.vector
+    t = g.tensor
+    near, far, rel, e_off, e_on, e_all = sides(cores, r, topo)
     own = T["win%d" % r]
 
-    g.sync.dma_start(T.hsall[r], T.hs[:, :]).then_inc(S.hsl, 16)
-    g.scalar.dma_start(own[:, :], T.mat[:, :]).then_inc(S.matl, 16)
+    g.sync.dma_start(T.hd[:, :], T.hs[:, :]).then_inc(S.hsl, 16)
+    if r == 0:
+        for k in range(NR):
+            for c in range(4):
+                (g.sync, g.scalar)[c % 2].dma_start(T.t0[k, 32 * c:32 * c + 32, :],
+                                                    T.mat[c::16, k * QW:(k + 1) * QW]).then_inc(S.pk, 16)
+        spread(T, lambda c: T.mat[c::16, :], own, (g.sync, g.scalar), S.w0)
+    else:
+        g.scalar.dma_start(own[:, 0:H], T.mat[:, 0:H]).then_inc(S.mata, 16)
+        g.scalar.dma_start(own[:, H:D], T.mat[:, H:D]).then_inc(S.matb, 16)
     g.sync.dma_start(T.idt[:, :], T.ids[:, :]).then_inc(S.idl, 16)
+    g.sync.dma_start(T.hx[:, 2 * r:2 * r + 2], T.hs[:, :]).then_inc(S.hxl, 16)
 
     g.iota(T.pi[:, 0:1], [[0, 1]], 0, 1).then_inc(S.iot, 1)
     g.iota(T.mq[:, :], [[1, 32], [0, 4]], 0, 0, allow_small_or_imprecise_dtypes=True).then_inc(S.iot, 1)
     g.iota(T.my[:, :], [[1, 32]], 0, 0, allow_small_or_imprecise_dtypes=True).then_inc(S.iot, 1)
-    g.wait_ge(S.hsl, 16)
-    g.remote_dma_fused([
-        RemoteDMATransfer(dst_ids=[dst(topo, c) for c in far], dma_engine_mask=bits(e_off), remote_sem=S.hsarr,
-                          srcs=[T.hsall[r]], dsts=[T.hsall[r] for c in far]),
-        RemoteDMATransfer(dst_ids=[dst(topo, c) for c in near], dma_engine_mask=bits(e_on), remote_sem=S.hsarr,
-                          srcs=[T.hsall[r]], dsts=[T.hsall[r] for c in near])], local_sem=S.sent)
-    g.wait_ge(S.matl, 16)
+    n = 0
+    hfar, hnear = hash_cores(cores, r, topo)
+    full = {"hsl": 16, "mata": 16, "matb": 16, "pk": 256, "w0": 256}
+    for x in ["hsl", [([hfar], e_off, "ha", 0, "hfar"), ([hnear], e_on, "hb", 0, "hnear")]] + plan(cores, r, topo):
+        if isinstance(x, list):
+            n += send(g, T, topo, x, {"hfar": "hd", "t0": "t0"}.get(x[0][4], "win%d" % r))
+        else:
+            g.wait_ge(S[x], full[x])
+    for q in FORWARD:
+        if core == forwarder(cores, q, topo):
+            g.wait_ge(S["fst%d" % q], count(cores, topo, "fst%d" % q, core))
+            n += send(g, T, topo, forwards(cores, q, topo), "win%d" % q)
+    g.wait_ge(S.sent, n)
 
-    def send_off():
-        g.remote_dma_fused([RemoteDMATransfer(
-            dst_ids=[dst(topo, rel[k])], dma_engine_mask=bits(e_off[2 * k:2 * k + 2]), remote_sem=S["ra%d" % r],
-            srcs=[own[:, k * QW:(k + 1) * QW]], dsts=[T["rl%d" % r][:, :]]) for k in range(NR)], local_sem=S.sent)
-
-    def send_on():
-        g.remote_dma_fused([RemoteDMATransfer(
-            dst_ids=[dst(topo, c) for c in near], dma_engine_mask=bits(e_on), remote_sem=S["tab%d" % r],
-            srcs=[own[:, :]], dsts=[own[:, :] for c in near])], local_sem=S.sent)
-
-    if r == 2:
-        send_on()
-        send_off()
-    else:
-        send_off()
-        send_on()
-    g.wait_ge(S.sent, 2 * (len(e_off) + len(e_on)))
-
-    g.sync.wait_ge(S.hsl, 16)
-    g.sync.wait_ge(S.hsarr, len(e_off) * len(far) + len(e_on) * len(near))
-    g.sync.dma_start(T.hrow[0:N, :], T.hsall[:, :, :]).then_inc(S.hl, 16)
-
-    v = g.vector
     nc = [0]
 
     def c(ins):
@@ -147,101 +240,82 @@ def rank_program(g, core, T, topo):
     v.wait_ge(S.iot, 3)
     c(v.tensor_scalar(T.pg[:, 0:1], T.pi[:, 0:1], 2, 28, A.logical_shift_right, A.bitwise_and))
     c(v.tensor_scalar(T.pc[:, 0:1], T.pi[:, 0:1], 3, None, A.bitwise_and))
-    c(v.tensor_scalar(T.pa[:, 0:1], T.pi[:, 0:1], 2, 3, A.logical_shift_right, A.bitwise_and))
-    c(v.tensor_copy(T.pf[:, 0:1], T.pi[:, 0:1]))
     v.wait_ge(S.cst, nc[0])
     c(v.tensor_tensor(T.key[:, 0:1], T.pg[:, 0:1], T.pc[:, 0:1], A.add))
-    c(v.tensor_scalar(T.pa2[:, 0:1], T.pa[:, 0:1], 100.0, None, A.mult))
-    c(v.tensor_scalar(T.eye[0:N, 0:N], T.my[0:N, 0:N], T.pf[0:N, 0:1], None, A.is_equal))
     v.wait_ge(S.cst, nc[0])
-    c(v.tensor_tensor(T.key0[:, 0:1], T.key[:, 0:1], T.pa2[:, 0:1], A.add))
     c(v.tensor_scalar(T.wm[:, :], T.mq[:, :], T.key[:, 0:1], None, A.is_equal))
     c(v.tensor_scalar(T.wy[:, :], T.my[:, :], T.key[:, 0:1], None, A.is_equal))
-    v.wait_ge(S.cst, nc[0])
-    c(v.tensor_scalar(T.ws[:, :], T.mq[:, :], T.key0[:, 0:1], None, A.is_equal))
-    ncst = nc[0]
+    t.wait_ge(S.cst, nc[0])
 
-    v.wait_ge(S.hl, 16)
-    v.tensor_copy(T.hta[0:N, :], T.hrow[0:N, 0::2]).then_inc(S.hcv, 1)
-    v.tensor_copy(T.htb[0:N, :], T.hrow[0:N, 1::2]).then_inc(S.hcv, 1)
-    g.tensor.wait_ge(S.cst, ncst)
-    g.tensor.wait_ge(S.hcv, 2)
-    g.tensor.matmul(T.psh[:, 0:N], T.hta[0:N, :], T.eye[0:N, 0:N], True, True).then_inc(S.hps, 1)
-    g.tensor.matmul(T.psh[:, 8:8 + N], T.htb[0:N, :], T.eye[0:N, 0:N], True, True).then_inc(S.hps, 1)
     v.wait_ge(S.idl, 16)
-    v.wait_ge(S.hps, 2)
-    L = K // 16
+    v.wait_ge(S.hxl, 16)
+    v.wait_ge(S.hsarr, (N - 1) * len(e_all))
+    v.tensor_copy(T.hf[:, :], T.hx[:, :]).then_inc(S.hcv, 1)
+    v.wait_ge(S.hcv, 1)
     for q in range(N):
-        v.tensor_scalar(T.xi[:, q * L:(q + 1) * L], T.idt[:, :], T.psh[:, q:q + 1], T.psh[:, 8 + q:9 + q],
+        v.tensor_scalar(T.xi[:, q * L:(q + 1) * L], T.idt[:, :], T.hf[:, 2 * q:2 * q + 1], T.hf[:, 2 * q + 1:2 * q + 2],
                         A.mult, A.add).then_inc(S.lst, 1)
     v.wait_ge(S.lst, N)
     v.tensor_scalar(T.xj[:, :], T.xi[:, :], 5, D - 1, A.logical_shift_right, A.bitwise_and).then_inc(S.lst, 1)
     v.wait_ge(S.lst, N + 1)
     v.tensor_copy(T.off[:, :], T.xj[:, :]).then_inc(S.lst, 1)
 
-    arrive = {}
-    for q in range(N):
+    def here(eng, q):
         if q == r:
-            arrive[q] = (S.matl, 16)
-        elif cores[q] in near:
-            arrive[q] = (S["tab%d" % q], len(e_on))
+            for s in (("w0",) if r == 0 else ("mata", "matb")):
+                eng.wait_ge(S[s], full[s])
         else:
-            arrive[q] = (S["tab%d" % q], NR * len(topo.engines(rel[0], far[0])))
-    LB = BW // 16
+            for s in ("fst%d" % q, "tab%d" % q):
+                k = count(cores, topo, s, core)
+                if k:
+                    eng.wait_ge(S[s], k)
 
-    def pick(eng, q, b):
-        eng.wait_ge(*arrive[q])
-        o = T["gat%d" % q][:, b * BW:(b + 1) * BW]
-        i = T["win%d" % q][:, :].indirect(T.off[:, q * L + b * LB:q * L + (b + 1) * LB])
-        if eng is g.scalar:
-            eng.activation(o, i, ActivationFunctionType.Copy).then_inc(S["gs%d_%d" % (q, b)], 1)
-        else:
-            eng.tensor_copy(o, i).then_inc(S["gs%d_%d" % (q, b)], 1)
+    def picked(q, b):
+        return T["win%d" % q][:, :].indirect(T.off[:, q * L + b * LB:q * L + (b + 1) * LB])
 
-    onchip = [q for q in range(N) if cores[q] in near]
     if r in (0, 1, 2):
-        order = [r] + [q for q in range(N) if q != r and not (q == 1)]
-        vq = 1 if r != 1 else None
+        order = [0, 2, 3, 4, 5]
     else:
-        order = [r, onchip[0], 0, 2] + [onchip[1]]
-        vq = 1
+        o = [q for q in (3, 4, 5) if q != r]
+        order = [r, 0, o[0], 2, o[1]]
     g.scalar.wait_ge(S.lst, N + 2)
     for q in order:
+        here(g.scalar, q)
         for b in range(NB):
-            pick(g.scalar, q, b)
+            g.scalar.activation(T["gat%d" % q][:, b * BW:(b + 1) * BW], picked(q, b),
+                                ActivationFunctionType.Copy).then_inc(S["gs%d_%d" % (q, b)], 1)
 
-    t = g.tensor
-    for b in range(NB):
-        t.wait_ge(S["gs0_%d" % b], 1)
-        t.matmul(T["v%d" % b][:, 0:BW], T.ws[:, :], T.gat0[:, b * BW:(b + 1) * BW], True, True).then_inc(S["pe%d" % b], 1)
     for q in range(1, N):
         for b in range(NB):
             t.wait_ge(S["dv%d" % b], q)
             if q < N - 1:
-                t.matmul(T["v%d" % b][:, 0:BW], T.wm[:, :], T["prod%d" % b][:, :], True, True).then_inc(S["pe%d" % b], 1)
+                o, w = T["v%d" % b][:, 0:BW], T.wm[:, :]
             else:
-                t.matmul(T["v%d" % b][0:32, 0:BW], T.wy[:, :], T["prod%d" % b][:, :], True, True).then_inc(S["pe%d" % b], 1)
+                o, w = T["v%d" % b][0:32, 0:BW], T.wy[:, :]
+            t.matmul(o, w, T["prod%d" % b][:, :], True, True).then_inc(S["pe%d" % b], 1)
     v.wait_ge(S.lst, N + 2)
-    for q in range(1, N):
+    here(v, 1)
+    for b in range(NB):
+        v.wait_ge(S["gs0_%d" % b], 1)
+        v.tensor_tensor(T["prod%d" % b][:, :], picked(1, b), T.gat0[:, b * BW:(b + 1) * BW],
+                        A.mult).then_inc(S["dv%d" % b], 1)
+    for q in range(2, N):
         for b in range(NB):
-            if q == vq:
-                pick(v, q, b)
             v.wait_ge(S["gs%d_%d" % (q, b)], 1)
-            v.wait_ge(S["pe%d" % b], q)
+            v.wait_ge(S["pe%d" % b], q - 1)
             v.tensor_tensor(T["prod%d" % b][:, :], T["v%d" % b][:, 0:BW], T["gat%d" % q][:, b * BW:(b + 1) * BW],
                             A.mult).then_inc(S["dv%d" % b], 1)
 
     for b in range(NB):
-        cols = slice(b * BW, (b + 1) * BW)
-        e = g.scalar if b % 2 == 0 else v
-        e.wait_ge(S["pe%d" % b], N)
+        cs = slice(b * BW, (b + 1) * BW)
+        yc = S["yc%d" % b]
         if b % 2 == 0:
-            e.activation(T.ysb[0:32, cols], T["v%d" % b][0:32, 0:BW], ActivationFunctionType.Copy).then_inc(S.yc, 1)
+            g.scalar.wait_ge(S["pe%d" % b], N - 1)
+            g.scalar.activation(T.ysb[0:32, cs], T["v%d" % b][0:32, 0:BW], ActivationFunctionType.Copy).then_inc(yc, 1)
         else:
-            e.tensor_copy(T.ysb[0:32, cols], T["v%d" % b][0:32, 0:BW]).then_inc(S.stored, 1)
-    g.scalar.wait_ge(S.yc, 1)
-    g.scalar.dma_start(T.y[:, 0:BW], T.ysb[0:32, 0:BW]).then_inc(S.yc, 16)
-    g.sync.wait_ge(S.stored, 1)
-    g.sync.dma_start(T.y[:, BW:K], T.ysb[0:32, BW:K]).then_inc(S.stored, 16)
-    g.scalar.wait_ge(S.yc, 17)
-    g.sync.wait_ge(S.stored, 17)
+            v.wait_ge(S["pe%d" % b], N - 1)
+            v.tensor_copy(T.ysb[0:32, cs], T["v%d" % b][0:32, 0:BW]).then_inc(yc, 1)
+        g.sync.wait_ge(yc, 1)
+        g.sync.dma_start(T.y[:, cs], T.ysb[0:32, cs]).then_inc(yc, 16)
+    for b in range(NB):
+        g.sync.wait_ge(S["yc%d" % b], 17)

@@ -5,44 +5,54 @@ N, D, K = 6, 2048, 1024
 NR = 4
 QW = D // NR
 H = D // 2
+PW = D // 4
 NB = 4
 BW = K // NB
 L = K // 16
 LB = BW // 16
+YB = BW // 4
 FORWARD = {1: [0], 2: [0, 1], 5: [0, 1]}
 
 SCRATCH = {
     "idt": ("sbuf", [128, L], "int32"),
+    "idp": ("sbuf", [128, L], "int32"),
     "hd": ("dram", [128, 2], "int32"),
     "hfar": ("dram", [128, 2], "int32"),
     "hnear": ("dram", [128, 2], "int32"),
-    "t0": ("dram", [NR, 128, 128], "bfloat16"),
+    "t0": ("dram", [128, PW], "bfloat16"),
     "hx": ("sbuf", [128, 2 * N], "int32"),
     "hf": ("sbuf", [128, 2 * N], "float32"),
     "xi": ("sbuf", [128, N * L], "int32"),
-    "xj": ("sbuf", [128, N * L], "int32"),
-    "off": ("sbuf", [128, N * L], "uint16"),
+    "xj": ("sbuf", [128, (N + 1) * L], "int32"),
+    "off": ("sbuf", [128, (N + 1) * L], "uint16"),
     "pi": ("sbuf", [128, 8], "int32"),
     "pg": ("sbuf", [128, 8], "int32"),
     "pc": ("sbuf", [128, 8], "int32"),
+    "pq": ("sbuf", [128, 8], "int32"),
     "key": ("sbuf", [128, 8], "float32"),
+    "kc": ("sbuf", [128, 8], "float32"),
+    "kq": ("sbuf", [128, 8], "float32"),
     "mq": ("sbuf", [128, 128], "float32"),
     "my": ("sbuf", [128, 32], "float32"),
     "wm": ("sbuf", [128, 128], "float32"),
     "wy": ("sbuf", [128, 32], "float32"),
-    "ysb": ("sbuf", [128, K], "float32"),
+    "ws": ("sbuf", [128, 128], "bfloat16"),
+    "oneh": ("sbuf", [128, 32], "bfloat16"),
+    "mask": ("sbuf", [128, K], "bfloat16"),
+    "ysb": ("sbuf", [128, K // 4], "float32"),
+    "win0": ("sbuf", [128, PW], "bfloat16"),
 }
-for _q in range(N):
+for _q in range(1, N):
     SCRATCH["win%d" % _q] = ("sbuf", [128, D], "bfloat16")
     SCRATCH["rl%d" % _q] = ("sbuf", [128, QW], "bfloat16")
-    if _q != 1:
-        SCRATCH["gat%d" % _q] = ("sbuf", [128, K], "bfloat16")
+    SCRATCH["gat%d" % _q] = ("sbuf", [128, K], "bfloat16")
 for _b in range(NB):
+    SCRATCH["first%d" % _b] = ("sbuf", [128, BW], "bfloat16")
     SCRATCH["prod%d" % _b] = ("sbuf", [128, BW], "float32")
     SCRATCH["v%d" % _b] = ("psum", [128, 512], "float32")
 
-SEMAPHORES = ["hsl", "hxl", "idl", "mata", "matb", "pk", "w0", "ha", "hb", "hsarr", "sent", "iot", "cst", "hcv", "lst"]
-SEMAPHORES += ["%s%d" % (s, q) for q in range(N) for s in ("tab", "fst", "ra")]
+SEMAPHORES = ["hsl", "hxl", "idl", "mata", "matb", "pk", "w0", "ha", "hb", "sent", "iot", "cst", "idc", "hcv", "lst", "ys"]
+SEMAPHORES += ["%s%d" % (s, q) for q in range(N) for s in ("tab", "fst", "ra", "hq", "lo")]
 SEMAPHORES += ["gs%d_%d" % (q, b) for q in range(N) for b in range(NB)]
 SEMAPHORES += ["%s%d" % (s, b) for b in range(NB) for s in ("pe", "dv", "yc")]
 
@@ -61,6 +71,10 @@ def helpers(cores, c, topo):
     return [x for x in idle if topo.die(x) == 1][:NR // 2] + [x for x in idle if topo.die(x) == 0][:NR // 2]
 
 
+def fifth(cores, c, topo):
+    return [x for x in topo.cores_of(c) if x not in cores and x not in helpers(cores, c, topo)][0]
+
+
 def cols(k):
     return (k * QW, (k + 1) * QW)
 
@@ -73,8 +87,7 @@ def plan(cores, q, topo):
         return ([rel[k]], es, ra, cols(k), rl)
 
     if q == 0:
-        return ["pk", [([rel[k]], e_off[2 * k:2 * k + 2], ra, k, "t0") for k in range(NR)],
-                "w0", [(near, e_on, tab, (0, H), win)], [(near, e_all, tab, (H, D), win)]]
+        return ["pk", [([fifth(cores, far[0], topo)], e_off, ra, (0, PW), "t0"), (near, e_on, tab, (0, PW), win)]]
     if q == 1:
         f = forwarder(cores, q, topo)
         o = [c for c in near if c != f]
@@ -105,13 +118,16 @@ def forwards(cores, q, topo):
 
 def hand_on(cores, q, k, topo):
     near, far, rel, e_off, e_on, e_all = sides(cores, q, topo)
+    if q == 0:
+        f = fifth(cores, far[0], topo)
+        return [(far, topo.engines(f, far[0]), "tab0", (0, PW), "win0")]
     return [(far, topo.engines(rel[k], far[0]), "tab%d" % q, cols(k), "win%d" % q)]
 
 
 def hash_cores(cores, q, topo):
-    near, far = sides(cores, q, topo)[:2]
+    near, far, rel = sides(cores, q, topo)[:3]
     i = sorted(near + [cores[q]]).index(cores[q])
-    return helpers(cores, far[0], topo)[i], helpers(cores, cores[q], topo)[i + 1]
+    return rel[i], helpers(cores, cores[q], topo)[i + 1]
 
 
 def count(cores, topo, sem, core):
@@ -119,7 +135,7 @@ def count(cores, topo, sem, core):
     for q in range(N):
         calls = [x for x in plan(cores, q, topo) if isinstance(x, list)]
         calls += [forwards(cores, q, topo)] if q in FORWARD else []
-        calls += [hand_on(cores, q, k, topo) for k in range(NR)]
+        calls += [hand_on(cores, q, k, topo) for k in range(NR if q else 1)]
         for call in calls:
             n += sum(len(x[1]) for x in call if x[2] == sem and core in x[0])
     return n
@@ -138,9 +154,7 @@ def bits(engines):
 
 
 def part(T, buf, where):
-    if buf == "t0":
-        return T.t0[where]
-    if buf[:2] == "rl" or buf in ("hd", "hfar", "hnear"):
+    if buf[:2] == "rl" or buf in ("hd", "hfar", "hnear", "t0"):
         return T[buf][:, :]
     return T[buf][:, where[0]:where[1]]
 
@@ -148,44 +162,43 @@ def part(T, buf, where):
 def send(g, T, topo, call, src):
     g.remote_dma_fused([RemoteDMATransfer(
         dst_ids=[dst(topo, c) for c in to], dma_engine_mask=bits(es), remote_sem=T.sem[sem],
-        srcs=[part(T, src, where)], dsts=[part(T, buf, where) for c in to])
+        srcs=[part(T, src(buf), where)], dsts=[part(T, buf, where) for c in to])
         for to, es, sem, where, buf in call], local_sem=T.sem.sent)
     return sum(len(x[1]) for x in call)
-
-
-def spread(T, table, win, queues, sem):
-    for c in range(4):
-        for i in range(4):
-            queues[i % 2].dma_start(win[4 * c + i::16, :], table(c)).then_inc(sem, 16)
 
 
 def relay_program(g, core, T, topo):
     cores = list(T.cores)
     S = T.sem
     if core not in helpers(cores, core, topo):
+        if core in plan(cores, 0, topo)[1][0][0]:
+            g.wait_ge(S.ra0, count(cores, topo, "ra0", core))
+            g.wait_ge(S.sent, send(g, T, topo, hand_on(cores, 0, 0, topo), lambda buf: "t0"))
         return
     n = 0
-    for near in (True, False):
-        for q in range(N):
+    for q in range(N):
+        for near in (True, False):
             if core == hash_cores(cores, q, topo)[1 if near else 0]:
                 to = [c for c in cores if topo.chip(c) == topo.chip(core) and c != cores[q]]
-                es = topo.engines(core, to[0])
-                qr = sides(cores, q, topo)
-                g.wait_ge(S.hb if near else S.ha, len(qr[4] if near else qr[3]))
-                n += send(g, T, topo, [(to, es, "hsarr", (2 * q, 2 * q + 2), "hx")], "hnear" if near else "hfar")
-    for q in range(N):
+                g.wait_ge(S.hb if near else S.ha, 1)
+                n += send(g, T, topo, [(to, topo.engines(core, to[0]), "hq%d" % q, (2 * q, 2 * q + 2), "hx")],
+                          lambda buf: "hnear" if near else "hfar")
+    for q in range(1, N):
         rel = sides(cores, q, topo)[2]
         if core in rel:
-            k = rel.index(core)
-            if q == 0:
-                for e in (g.sync, g.scalar):
-                    e.wait_ge(S.ra0, count(cores, topo, "ra0", core))
-                spread(T, lambda c: T.t0[k, 32 * c:32 * c + 32, :], T.rl0, (g.sync, g.scalar), S.w0)
-                g.wait_ge(S.w0, 256)
-            else:
-                g.wait_ge(S["ra%d" % q], count(cores, topo, "ra%d" % q, core))
-            n += send(g, T, topo, hand_on(cores, q, k, topo), "rl%d" % q)
+            g.wait_ge(S["ra%d" % q], count(cores, topo, "ra%d" % q, core))
+            n += send(g, T, topo, hand_on(cores, q, rel.index(core), topo), lambda buf: "rl%d" % q)
     g.wait_ge(S.sent, n)
+
+
+def runs(modes):
+    out = []
+    for q in sorted(modes):
+        if out and out[-1][1] == q:
+            out[-1][1] = q + 1
+        else:
+            out.append([q, q + 1])
+    return out
 
 
 def rank_program(g, core, T, topo):
@@ -201,13 +214,12 @@ def rank_program(g, core, T, topo):
     near, far, rel, e_off, e_on, e_all = sides(cores, r, topo)
     own = T["win%d" % r]
 
-    g.sync.dma_start(T.hd[:, :], T.hs[:, :]).then_inc(S.hsl, 16)
+    g.scalar.dma_start(T.hd[:, :], T.hs[:, :]).then_inc(S.hsl, 16)
     if r == 0:
-        for k in range(NR):
-            for c in range(4):
-                (g.sync, g.scalar)[c % 2].dma_start(T.t0[k, 32 * c:32 * c + 32, :],
-                                                    T.mat[c::16, k * QW:(k + 1) * QW]).then_inc(S.pk, 16)
-        spread(T, lambda c: T.mat[c::16, :], own, (g.sync, g.scalar), S.w0)
+        for buf, sem in ((T.t0, S.pk), (own, S.w0)):
+            for k in range(8):
+                (g.scalar, g.sync)[k % 2].dma_start(buf[16 * k:16 * k + 16, :],
+                                                    T.mat[16 * k:16 * k + 4, :]).then_inc(sem, 16)
     else:
         g.scalar.dma_start(own[:, 0:H], T.mat[:, 0:H]).then_inc(S.mata, 16)
         g.scalar.dma_start(own[:, H:D], T.mat[:, H:D]).then_inc(S.matb, 16)
@@ -218,17 +230,18 @@ def rank_program(g, core, T, topo):
     g.iota(T.mq[:, :], [[1, 32], [0, 4]], 0, 0, allow_small_or_imprecise_dtypes=True).then_inc(S.iot, 1)
     g.iota(T.my[:, :], [[1, 32]], 0, 0, allow_small_or_imprecise_dtypes=True).then_inc(S.iot, 1)
     n = 0
+    full = {"hsl": 16, "mata": 16, "matb": 16, "pk": 128, "w0": 128}
     hfar, hnear = hash_cores(cores, r, topo)
-    full = {"hsl": 16, "mata": 16, "matb": 16, "pk": 256, "w0": 256}
-    for x in ["hsl", [([hfar], e_off, "ha", 0, "hfar"), ([hnear], e_on, "hb", 0, "hnear")]] + plan(cores, r, topo):
+    hashes = [([hfar], e_off[:1], "ha", 0, "hfar"), ([hnear], e_on[:1], "hb", 0, "hnear")]
+    for x in ["hsl", hashes] + plan(cores, r, topo):
         if isinstance(x, list):
-            n += send(g, T, topo, x, {"hfar": "hd", "t0": "t0"}.get(x[0][4], "win%d" % r))
+            n += send(g, T, topo, x, lambda buf: {"hfar": "hd", "hnear": "hd"}.get(buf, "win%d" % r if r else "t0"))
         else:
             g.wait_ge(S[x], full[x])
     for q in FORWARD:
         if core == forwarder(cores, q, topo):
             g.wait_ge(S["fst%d" % q], count(cores, topo, "fst%d" % q, core))
-            n += send(g, T, topo, forwards(cores, q, topo), "win%d" % q)
+            n += send(g, T, topo, forwards(cores, q, topo), lambda buf: "win%d" % q)
     g.wait_ge(S.sent, n)
 
     nc = [0]
@@ -240,27 +253,73 @@ def rank_program(g, core, T, topo):
     v.wait_ge(S.iot, 3)
     c(v.tensor_scalar(T.pg[:, 0:1], T.pi[:, 0:1], 2, 28, A.logical_shift_right, A.bitwise_and))
     c(v.tensor_scalar(T.pc[:, 0:1], T.pi[:, 0:1], 3, None, A.bitwise_and))
+    c(v.tensor_scalar(T.pq[:, 0:1], T.pi[:, 0:1], 2, None, A.logical_shift_right))
     v.wait_ge(S.cst, nc[0])
     c(v.tensor_tensor(T.key[:, 0:1], T.pg[:, 0:1], T.pc[:, 0:1], A.add))
+    c(v.tensor_copy(T.kc[:, 0:1], T.pc[:, 0:1]))
+    c(v.tensor_copy(T.kq[:, 0:1], T.pq[:, 0:1]))
     v.wait_ge(S.cst, nc[0])
+    c(v.tensor_scalar(T.oneh[:, :], T.my[:, :], T.kc[:, 0:1], None, A.is_equal))
+    c(v.tensor_scalar(T.ws[:, :], T.mq[:, :], T.kq[:, 0:1], None, A.is_equal))
     c(v.tensor_scalar(T.wm[:, :], T.mq[:, :], T.key[:, 0:1], None, A.is_equal))
     c(v.tensor_scalar(T.wy[:, :], T.my[:, :], T.key[:, 0:1], None, A.is_equal))
     t.wait_ge(S.cst, nc[0])
+    g.scalar.wait_ge(S.cst, nc[0])
 
     v.wait_ge(S.idl, 16)
-    v.wait_ge(S.hxl, 16)
-    v.wait_ge(S.hsarr, (N - 1) * len(e_all))
-    v.tensor_copy(T.hf[:, :], T.hx[:, :]).then_inc(S.hcv, 1)
-    v.wait_ge(S.hcv, 1)
-    for q in range(N):
-        v.tensor_scalar(T.xi[:, q * L:(q + 1) * L], T.idt[:, :], T.hf[:, 2 * q:2 * q + 1], T.hf[:, 2 * q + 1:2 * q + 2],
-                        A.mult, A.add).then_inc(S.lst, 1)
-    v.wait_ge(S.lst, N)
-    v.tensor_scalar(T.xj[:, :], T.xi[:, :], 5, D - 1, A.logical_shift_right, A.bitwise_and).then_inc(S.lst, 1)
-    v.wait_ge(S.lst, N + 1)
-    v.tensor_copy(T.off[:, :], T.xj[:, :]).then_inc(S.lst, 1)
+    for a in range(4):
+        for i in range(2):
+            v.tensor_copy(T.idp[:, 2 * a + i::8], T.idt[:, 16 * a + i:16 * a + 16:2]).then_inc(S.idc, 1)
+    v.wait_ge(S.idc, 8)
+
+    nl = [0, 0]
+    ready = {}
+
+    def lists(modes):
+        for q in modes:
+            if q == r:
+                v.wait_ge(S.hxl, 16)
+            else:
+                v.wait_ge(S["hq%d" % q], len(e_all))
+        rs = runs(modes)
+        for a, b in rs:
+            nl[0] += 1
+            v.tensor_copy(T.hf[:, 2 * a:2 * b], T.hx[:, 2 * a:2 * b]).then_inc(S.hcv, 1)
+        yield
+        v.wait_ge(S.hcv, nl[0])
+        for q in modes:
+            nl[1] += 1
+            v.tensor_scalar(T.xi[:, q * L:(q + 1) * L], T.idp[:, :], T.hf[:, 2 * q:2 * q + 1],
+                            T.hf[:, 2 * q + 1:2 * q + 2], A.mult, A.add).then_inc(S.lst, 1)
+        yield
+        v.wait_ge(S.lst, nl[1])
+        for a, b in rs:
+            cuts = [(0, a, b, 5, D - 1)] if a else [(-1, 0, 1, 14, 3), (0, 0, 1, 5, PW - 1), (0, 1, b, 5, D - 1)]
+            for d, i, j, shift, mask in cuts:
+                if i < j:
+                    nl[1] += 1
+                    v.tensor_scalar(T.xj[:, (i + 1 + d) * L:(j + 1 + d) * L], T.xi[:, i * L:j * L], shift, mask,
+                                    A.logical_shift_right, A.bitwise_and).then_inc(S.lst, 1)
+        yield
+        v.wait_ge(S.lst, nl[1])
+        for a, b in rs:
+            i = a + 1 if a else 0
+            v.tensor_copy(T.off[:, i * L:(b + 1) * L], T.xj[:, i * L:(b + 1) * L]).then_inc(S["lo%d" % a], 1)
+            for q in range(a, b):
+                ready[q] = S["lo%d" % a]
+        yield
+
+    def several(groups):
+        for modes in groups:
+            for _ in lists(modes):
+                yield
+
+    def go_on(steps):
+        for _ in range(steps):
+            next(later, None)
 
     def here(eng, q):
+        eng.wait_ge(ready[q], 1)
         if q == r:
             for s in (("w0",) if r == 0 else ("mata", "matb")):
                 eng.wait_ge(S[s], full[s])
@@ -270,52 +329,60 @@ def rank_program(g, core, T, topo):
                 if k:
                     eng.wait_ge(S[s], k)
 
-    def picked(q, b):
-        return T["win%d" % q][:, :].indirect(T.off[:, q * L + b * LB:q * L + (b + 1) * LB])
+    def picked(win, i, b):
+        return win[:, :].indirect(T.off[:, i * L + b * LB:i * L + (b + 1) * LB])
 
-    if r in (0, 1, 2):
-        order = [0, 2, 3, 4, 5]
-    else:
-        o = [q for q in (3, 4, 5) if q != r]
-        order = [r, 0, o[0], 2, o[1]]
-    g.scalar.wait_ge(S.lst, N + 2)
-    for q in order:
-        here(g.scalar, q)
-        for b in range(NB):
-            g.scalar.activation(T["gat%d" % q][:, b * BW:(b + 1) * BW], picked(q, b),
-                                ActivationFunctionType.Copy).then_inc(S["gs%d_%d" % (q, b)], 1)
-
-    for q in range(1, N):
-        for b in range(NB):
-            t.wait_ge(S["dv%d" % b], q)
-            if q < N - 1:
-                o, w = T["v%d" % b][:, 0:BW], T.wm[:, :]
-            else:
-                o, w = T["v%d" % b][0:32, 0:BW], T.wy[:, :]
-            t.matmul(o, w, T["prod%d" % b][:, :], True, True).then_inc(S["pe%d" % b], 1)
-    v.wait_ge(S.lst, N + 2)
-    here(v, 1)
+    start = [r, 0] if r else [0]
+    then = [q for q in range(N) if q not in start]
+    for _ in several([[q] for q in start]):
+        pass
+    later = several([then[:1], then[1:]])
+    go_on(2)
+    here(v, 0)
     for b in range(NB):
         v.wait_ge(S["gs0_%d" % b], 1)
-        v.tensor_tensor(T["prod%d" % b][:, :], picked(1, b), T.gat0[:, b * BW:(b + 1) * BW],
+        v.tensor_tensor(T["first%d" % b][:, :], picked(T.win0, 1, b), T.mask[:, b * BW:(b + 1) * BW],
                         A.mult).then_inc(S["dv%d" % b], 1)
-    for q in range(2, N):
+        go_on(1)
+    for q in range(1, N):
         for b in range(NB):
             v.wait_ge(S["gs%d_%d" % (q, b)], 1)
-            v.wait_ge(S["pe%d" % b], q - 1)
+            v.wait_ge(S["pe%d" % b], q)
             v.tensor_tensor(T["prod%d" % b][:, :], T["v%d" % b][:, 0:BW], T["gat%d" % q][:, b * BW:(b + 1) * BW],
                             A.mult).then_inc(S["dv%d" % b], 1)
+            go_on(1)
+
+    for q in sorted(range(N), key=lambda q: (q != r, q)):
+        if q:
+            here(g.scalar, q)
+        else:
+            g.scalar.wait_ge(ready[0], 1)
+        for b in range(NB):
+            out, win = (T["gat%d" % q], T["win%d" % q]) if q else (T.mask, T.oneh)
+            g.scalar.activation(out[:, b * BW:(b + 1) * BW], picked(win, q + 1 if q else 0, b),
+                                ActivationFunctionType.Copy).then_inc(S["gs%d_%d" % (q, b)], 1)
+
+    for q in range(N):
+        for b in range(NB):
+            t.wait_ge(S["dv%d" % b], q + 1)
+            pe = S["pe%d" % b]
+            if q == 0:
+                t.matmul(T["v%d" % b][:, 0:BW], T.ws[:, :], T["first%d" % b][:, :], True, True).then_inc(pe, 1)
+            elif q < N - 1:
+                t.matmul(T["v%d" % b][:, 0:BW], T.wm[:, :], T["prod%d" % b][:, :], True, True).then_inc(pe, 1)
+            else:
+                for i in range(BW // 128):
+                    t.matmul(T["v%d" % b][:, 32 * i:32 * i + 32], T["prod%d" % b][:, 128 * i:128 * i + 128], T.wy[:, :],
+                             True, True).then_inc(pe, 1)
 
     for b in range(NB):
-        cs = slice(b * BW, (b + 1) * BW)
-        yc = S["yc%d" % b]
-        if b % 2 == 0:
-            g.scalar.wait_ge(S["pe%d" % b], N - 1)
-            g.scalar.activation(T.ysb[0:32, cs], T["v%d" % b][0:32, 0:BW], ActivationFunctionType.Copy).then_inc(yc, 1)
-        else:
-            v.wait_ge(S["pe%d" % b], N - 1)
-            v.tensor_copy(T.ysb[0:32, cs], T["v%d" % b][0:32, 0:BW]).then_inc(yc, 1)
-        g.sync.wait_ge(yc, 1)
-        g.sync.dma_start(T.y[:, cs], T.ysb[0:32, cs]).then_inc(yc, 16)
-    for b in range(NB):
-        g.sync.wait_ge(S["yc%d" % b], 17)
+        v.wait_ge(S["pe%d" % b], N - 1 + BW // 128)
+        v.transpose(T.ysb[:, b * YB:(b + 1) * YB], T["v%d" % b][:, 0:YB]).then_inc(S["yc%d" % b], 1)
+    for b0, b1 in ((0, NB - 1), (NB - 1, NB)):
+        for e in (g.sync, g.scalar):
+            for b in range(b0, b1):
+                e.wait_ge(S["yc%d" % b], 1)
+        for a in range(4):
+            (g.sync, g.scalar)[a % 2].dma_start(T.y[:, 256 * a + b0 * YB:256 * a + b1 * YB],
+                                                T.ysb[32 * a:32 * a + 32, b0 * YB:b1 * YB]).then_inc(S.ys, 16)
+    g.sync.wait_ge(S.ys, 128)

from concourse.bass import DstId, RemoteDMATransfer
from concourse.mybir import AluOpType, ActivationFunctionType

N, D, K = 6, 2048, 1024
NR = 4
QW = D // NR
H = D // 2
PW = D // 4
NB = 4
BW = K // NB
L = K // 16
LB = BW // 16
YB = BW // 4
FORWARD = {1: [0], 2: [0, 1], 5: [0, 1]}

SCRATCH = {
    "idt": ("sbuf", [128, L], "int32"),
    "idp": ("sbuf", [128, L], "int32"),
    "hd": ("dram", [128, 2], "int32"),
    "hfar": ("dram", [128, 2], "int32"),
    "hnear": ("dram", [128, 2], "int32"),
    "t0": ("dram", [128, PW], "bfloat16"),
    "hx": ("sbuf", [128, 2 * N], "int32"),
    "hf": ("sbuf", [128, 2 * N], "float32"),
    "xi": ("sbuf", [128, N * L], "int32"),
    "xj": ("sbuf", [128, (N + 1) * L], "int32"),
    "off": ("sbuf", [128, (N + 1) * L], "uint16"),
    "pi": ("sbuf", [128, 8], "int32"),
    "pg": ("sbuf", [128, 8], "int32"),
    "pc": ("sbuf", [128, 8], "int32"),
    "pq": ("sbuf", [128, 8], "int32"),
    "key": ("sbuf", [128, 8], "float32"),
    "kc": ("sbuf", [128, 8], "float32"),
    "kq": ("sbuf", [128, 8], "float32"),
    "mq": ("sbuf", [128, 128], "float32"),
    "my": ("sbuf", [128, 32], "float32"),
    "wm": ("sbuf", [128, 128], "float32"),
    "wy": ("sbuf", [128, 32], "float32"),
    "ws": ("sbuf", [128, 128], "bfloat16"),
    "oneh": ("sbuf", [128, 32], "bfloat16"),
    "mask": ("sbuf", [128, K], "bfloat16"),
    "ysb": ("sbuf", [128, K // 4], "float32"),
    "win0": ("sbuf", [128, PW], "bfloat16"),
}
for _q in range(1, N):
    SCRATCH["win%d" % _q] = ("sbuf", [128, D], "bfloat16")
    SCRATCH["rl%d" % _q] = ("sbuf", [128, QW], "bfloat16")
    SCRATCH["gat%d" % _q] = ("sbuf", [128, K], "bfloat16")
for _b in range(NB):
    SCRATCH["first%d" % _b] = ("sbuf", [128, BW], "bfloat16")
    SCRATCH["prod%d" % _b] = ("sbuf", [128, BW], "float32")
    SCRATCH["v%d" % _b] = ("psum", [128, 512], "float32")

SEMAPHORES = ["hsl", "hxl", "idl", "mata", "matb", "pk", "w0", "ha", "hb", "sent", "iot", "cst", "idc", "hcv", "lst", "ys"]
SEMAPHORES += ["%s%d" % (s, q) for q in range(N) for s in ("tab", "fst", "ra", "hq", "lo")]
SEMAPHORES += ["gs%d_%d" % (q, b) for q in range(N) for b in range(NB)]
SEMAPHORES += ["%s%d" % (s, b) for b in range(NB) for s in ("pe", "dv", "yc")]


def sides(cores, q, topo):
    me = cores[q]
    near = [c for c in cores if c != me and topo.chip(c) == topo.chip(me)]
    far = [c for c in cores if topo.chip(c) != topo.chip(me)]
    e_off = topo.engines(me, far[0])
    e_all = topo.engines(me, near[0])
    return near, far, helpers(cores, far[0], topo), e_off, [e for e in e_all if e not in e_off], e_all


def helpers(cores, c, topo):
    idle = [x for x in topo.cores_of(c) if x not in cores]
    return [x for x in idle if topo.die(x) == 1][:NR // 2] + [x for x in idle if topo.die(x) == 0][:NR // 2]


def fifth(cores, c, topo):
    return [x for x in topo.cores_of(c) if x not in cores and x not in helpers(cores, c, topo)][0]


def cols(k):
    return (k * QW, (k + 1) * QW)


def plan(cores, q, topo):
    near, far, rel, e_off, e_on, e_all = sides(cores, q, topo)
    tab, fst, ra, win, rl = ["%s%d" % (s, q) for s in ("tab", "fst", "ra", "win", "rl")]

    def rp(k, es):
        return ([rel[k]], es, ra, cols(k), rl)

    if q == 0:
        return ["pk", [([fifth(cores, far[0], topo)], e_off, ra, (0, PW), "t0"), (near, e_on, tab, (0, PW), win)]]
    if q == 1:
        f = forwarder(cores, q, topo)
        o = [c for c in near if c != f]
        return ["mata", [rp(1, e_off), ([f], e_on, fst, cols(0), win)],
                "matb", [rp(2, e_off[:4]), rp(3, e_off[4:]), (near, e_on, tab, cols(1), win)],
                [(o, e_on, tab, cols(0), win)],
                [(near, e_all, tab, (H, D), win)]]
    if q in FORWARD:
        return ["mata", [(near, e_all, fst, (0, H), win)],
                "matb", [(near, e_all, tab, (H, D), win)],
                [rp(2, e_off[:4]), rp(3, e_off[4:])]]
    return ["mata", [rp(0, e_off[:4]), rp(1, e_off[4:])],
            [(near, e_on, tab, (0, H), win)],
            "matb", [rp(2, e_off[:4]), rp(3, e_off[4:])],
            [(near, e_all, tab, (H, D), win)]]


def forwarder(cores, q, topo):
    return [c for c in cores if topo.chip(c) == topo.chip(cores[q]) and topo.die(c) != topo.die(cores[q])][0]


def forwards(cores, q, topo):
    rel = sides(cores, q, topo)[2]
    es = topo.engines(forwarder(cores, q, topo), rel[0])
    w = len(es) // len(FORWARD[q])
    return [([rel[k]], es[w * i:w * i + w], "ra%d" % q, cols(k), "rl%d" % q) for i, k in enumerate(FORWARD[q])]


def hand_on(cores, q, k, topo):
    near, far, rel, e_off, e_on, e_all = sides(cores, q, topo)
    if q == 0:
        f = fifth(cores, far[0], topo)
        return [(far, topo.engines(f, far[0]), "tab0", (0, PW), "win0")]
    return [(far, topo.engines(rel[k], far[0]), "tab%d" % q, cols(k), "win%d" % q)]


def hash_cores(cores, q, topo):
    near, far, rel = sides(cores, q, topo)[:3]
    i = sorted(near + [cores[q]]).index(cores[q])
    return rel[i], helpers(cores, cores[q], topo)[i + 1]


def count(cores, topo, sem, core):
    n = 0
    for q in range(N):
        calls = [x for x in plan(cores, q, topo) if isinstance(x, list)]
        calls += [forwards(cores, q, topo)] if q in FORWARD else []
        calls += [hand_on(cores, q, k, topo) for k in range(NR if q else 1)]
        for call in calls:
            n += sum(len(x[1]) for x in call if x[2] == sem and core in x[0])
    return n


def dst(topo, c):
    a = topo.addr(c)
    return DstId(rid=a[0], pnc=a[1])


def bits(engines):
    m = 0
    for e in engines:
        m |= 1 << e
    return m


def part(T, buf, where):
    if buf[:2] == "rl" or buf in ("hd", "hfar", "hnear", "t0"):
        return T[buf][:, :]
    return T[buf][:, where[0]:where[1]]


def send(g, T, topo, call, src):
    g.remote_dma_fused([RemoteDMATransfer(
        dst_ids=[dst(topo, c) for c in to], dma_engine_mask=bits(es), remote_sem=T.sem[sem],
        srcs=[part(T, src(buf), where)], dsts=[part(T, buf, where) for c in to])
        for to, es, sem, where, buf in call], local_sem=T.sem.sent)
    return sum(len(x[1]) for x in call)


def relay_program(g, core, T, topo):
    cores = list(T.cores)
    S = T.sem
    if core not in helpers(cores, core, topo):
        if core in plan(cores, 0, topo)[1][0][0]:
            g.wait_ge(S.ra0, count(cores, topo, "ra0", core))
            g.wait_ge(S.sent, send(g, T, topo, hand_on(cores, 0, 0, topo), lambda buf: "t0"))
        return
    n = 0
    for q in range(N):
        for near in (True, False):
            if core == hash_cores(cores, q, topo)[1 if near else 0]:
                to = [c for c in cores if topo.chip(c) == topo.chip(core) and c != cores[q]]
                g.wait_ge(S.hb if near else S.ha, 1)
                n += send(g, T, topo, [(to, topo.engines(core, to[0]), "hq%d" % q, (2 * q, 2 * q + 2), "hx")],
                          lambda buf: "hnear" if near else "hfar")
    for q in range(1, N):
        rel = sides(cores, q, topo)[2]
        if core in rel:
            g.wait_ge(S["ra%d" % q], count(cores, topo, "ra%d" % q, core))
            n += send(g, T, topo, hand_on(cores, q, rel.index(core), topo), lambda buf: "rl%d" % q)
    g.wait_ge(S.sent, n)


def runs(modes):
    out = []
    for q in sorted(modes):
        if out and out[-1][1] == q:
            out[-1][1] = q + 1
        else:
            out.append([q, q + 1])
    return out


def rank_program(g, core, T, topo):
    r = T.rank_of(core)
    cores = list(T.cores)
    if r is None:
        relay_program(g, core, T, topo)
        return
    A = AluOpType
    S = T.sem
    v = g.vector
    t = g.tensor
    near, far, rel, e_off, e_on, e_all = sides(cores, r, topo)
    own = T["win%d" % r]

    g.scalar.dma_start(T.hd[:, :], T.hs[:, :]).then_inc(S.hsl, 16)
    if r == 0:
        for buf, sem in ((T.t0, S.pk), (own, S.w0)):
            for k in range(8):
                (g.scalar, g.sync)[k % 2].dma_start(buf[16 * k:16 * k + 16, :],
                                                    T.mat[16 * k:16 * k + 4, :]).then_inc(sem, 16)
    else:
        g.scalar.dma_start(own[:, 0:H], T.mat[:, 0:H]).then_inc(S.mata, 16)
        g.scalar.dma_start(own[:, H:D], T.mat[:, H:D]).then_inc(S.matb, 16)
    g.sync.dma_start(T.idt[:, :], T.ids[:, :]).then_inc(S.idl, 16)
    g.sync.dma_start(T.hx[:, 2 * r:2 * r + 2], T.hs[:, :]).then_inc(S.hxl, 16)

    g.iota(T.pi[:, 0:1], [[0, 1]], 0, 1).then_inc(S.iot, 1)
    g.iota(T.mq[:, :], [[1, 32], [0, 4]], 0, 0, allow_small_or_imprecise_dtypes=True).then_inc(S.iot, 1)
    g.iota(T.my[:, :], [[1, 32]], 0, 0, allow_small_or_imprecise_dtypes=True).then_inc(S.iot, 1)
    n = 0
    full = {"hsl": 16, "mata": 16, "matb": 16, "pk": 128, "w0": 128}
    hfar, hnear = hash_cores(cores, r, topo)
    hashes = [([hfar], e_off[:1], "ha", 0, "hfar"), ([hnear], e_on[:1], "hb", 0, "hnear")]
    for x in ["hsl", hashes] + plan(cores, r, topo):
        if isinstance(x, list):
            n += send(g, T, topo, x, lambda buf: {"hfar": "hd", "hnear": "hd"}.get(buf, "win%d" % r if r else "t0"))
        else:
            g.wait_ge(S[x], full[x])
    for q in FORWARD:
        if core == forwarder(cores, q, topo):
            g.wait_ge(S["fst%d" % q], count(cores, topo, "fst%d" % q, core))
            n += send(g, T, topo, forwards(cores, q, topo), lambda buf: "win%d" % q)
    g.wait_ge(S.sent, n)

    nc = [0]

    def c(ins):
        nc[0] += 1
        ins.then_inc(S.cst, 1)

    v.wait_ge(S.iot, 3)
    c(v.tensor_scalar(T.pg[:, 0:1], T.pi[:, 0:1], 2, 28, A.logical_shift_right, A.bitwise_and))
    c(v.tensor_scalar(T.pc[:, 0:1], T.pi[:, 0:1], 3, None, A.bitwise_and))
    c(v.tensor_scalar(T.pq[:, 0:1], T.pi[:, 0:1], 2, None, A.logical_shift_right))
    v.wait_ge(S.cst, nc[0])
    c(v.tensor_tensor(T.key[:, 0:1], T.pg[:, 0:1], T.pc[:, 0:1], A.add))
    c(v.tensor_copy(T.kc[:, 0:1], T.pc[:, 0:1]))
    c(v.tensor_copy(T.kq[:, 0:1], T.pq[:, 0:1]))
    v.wait_ge(S.cst, nc[0])
    c(v.tensor_scalar(T.oneh[:, :], T.my[:, :], T.kc[:, 0:1], None, A.is_equal))
    c(v.tensor_scalar(T.ws[:, :], T.mq[:, :], T.kq[:, 0:1], None, A.is_equal))
    c(v.tensor_scalar(T.wm[:, :], T.mq[:, :], T.key[:, 0:1], None, A.is_equal))
    c(v.tensor_scalar(T.wy[:, :], T.my[:, :], T.key[:, 0:1], None, A.is_equal))
    t.wait_ge(S.cst, nc[0])
    g.scalar.wait_ge(S.cst, nc[0])

    v.wait_ge(S.idl, 16)
    for a in range(4):
        for i in range(2):
            v.tensor_copy(T.idp[:, 2 * a + i::8], T.idt[:, 16 * a + i:16 * a + 16:2]).then_inc(S.idc, 1)
    v.wait_ge(S.idc, 8)

    nl = [0, 0]
    ready = {}

    def lists(modes):
        for q in modes:
            if q == r:
                v.wait_ge(S.hxl, 16)
            else:
                v.wait_ge(S["hq%d" % q], len(e_all))
        rs = runs(modes)
        for a, b in rs:
            nl[0] += 1
            v.tensor_copy(T.hf[:, 2 * a:2 * b], T.hx[:, 2 * a:2 * b]).then_inc(S.hcv, 1)
        yield
        v.wait_ge(S.hcv, nl[0])
        for q in modes:
            nl[1] += 1
            v.tensor_scalar(T.xi[:, q * L:(q + 1) * L], T.idp[:, :], T.hf[:, 2 * q:2 * q + 1],
                            T.hf[:, 2 * q + 1:2 * q + 2], A.mult, A.add).then_inc(S.lst, 1)
        yield
        v.wait_ge(S.lst, nl[1])
        for a, b in rs:
            cuts = [(0, a, b, 5, D - 1)] if a else [(-1, 0, 1, 14, 3), (0, 0, 1, 5, PW - 1), (0, 1, b, 5, D - 1)]
            for d, i, j, shift, mask in cuts:
                if i < j:
                    nl[1] += 1
                    v.tensor_scalar(T.xj[:, (i + 1 + d) * L:(j + 1 + d) * L], T.xi[:, i * L:j * L], shift, mask,
                                    A.logical_shift_right, A.bitwise_and).then_inc(S.lst, 1)
        yield
        v.wait_ge(S.lst, nl[1])
        for a, b in rs:
            i = a + 1 if a else 0
            v.tensor_copy(T.off[:, i * L:(b + 1) * L], T.xj[:, i * L:(b + 1) * L]).then_inc(S["lo%d" % a], 1)
            for q in range(a, b):
                ready[q] = S["lo%d" % a]
        yield

    def several(groups):
        for modes in groups:
            for _ in lists(modes):
                yield

    def go_on(steps):
        for _ in range(steps):
            next(later, None)

    def here(eng, q):
        eng.wait_ge(ready[q], 1)
        if q == r:
            for s in (("w0",) if r == 0 else ("mata", "matb")):
                eng.wait_ge(S[s], full[s])
        else:
            for s in ("fst%d" % q, "tab%d" % q):
                k = count(cores, topo, s, core)
                if k:
                    eng.wait_ge(S[s], k)

    def picked(win, i, b):
        return win[:, :].indirect(T.off[:, i * L + b * LB:i * L + (b + 1) * LB])

    start = [r, 0] if r else [0]
    then = [q for q in range(N) if q not in start]
    for _ in several([[q] for q in start]):
        pass
    later = several([then[:1], then[1:]])
    go_on(2)
    here(v, 0)
    for b in range(NB):
        v.wait_ge(S["gs0_%d" % b], 1)
        v.tensor_tensor(T["first%d" % b][:, :], picked(T.win0, 1, b), T.mask[:, b * BW:(b + 1) * BW],
                        A.mult).then_inc(S["dv%d" % b], 1)
        go_on(1)
    for q in range(1, N):
        for b in range(NB):
            v.wait_ge(S["gs%d_%d" % (q, b)], 1)
            v.wait_ge(S["pe%d" % b], q)
            v.tensor_tensor(T["prod%d" % b][:, :], T["v%d" % b][:, 0:BW], T["gat%d" % q][:, b * BW:(b + 1) * BW],
                            A.mult).then_inc(S["dv%d" % b], 1)
            go_on(1)

    for q in sorted(range(N), key=lambda q: (q != r, q)):
        if q:
            here(g.scalar, q)
        else:
            g.scalar.wait_ge(ready[0], 1)
        for b in range(NB):
            out, win = (T["gat%d" % q], T["win%d" % q]) if q else (T.mask, T.oneh)
            g.scalar.activation(out[:, b * BW:(b + 1) * BW], picked(win, q + 1 if q else 0, b),
                                ActivationFunctionType.Copy).then_inc(S["gs%d_%d" % (q, b)], 1)

    for q in range(N):
        for b in range(NB):
            t.wait_ge(S["dv%d" % b], q + 1)
            pe = S["pe%d" % b]
            if q == 0:
                t.matmul(T["v%d" % b][:, 0:BW], T.ws[:, :], T["first%d" % b][:, :], True, True).then_inc(pe, 1)
            elif q < N - 1:
                t.matmul(T["v%d" % b][:, 0:BW], T.wm[:, :], T["prod%d" % b][:, :], True, True).then_inc(pe, 1)
            else:
                for i in range(BW // 128):
                    t.matmul(T["v%d" % b][:, 32 * i:32 * i + 32], T["prod%d" % b][:, 128 * i:128 * i + 128], T.wy[:, :],
                             True, True).then_inc(pe, 1)

    for b in range(NB):
        v.wait_ge(S["pe%d" % b], N - 1 + BW // 128)
        v.transpose(T.ysb[:, b * YB:(b + 1) * YB], T["v%d" % b][:, 0:YB]).then_inc(S["yc%d" % b], 1)
    for b0, b1 in ((0, NB - 1), (NB - 1, NB)):
        for e in (g.sync, g.scalar):
            for b in range(b0, b1):
                e.wait_ge(S["yc%d" % b], 1)
        for a in range(4):
            (g.sync, g.scalar)[a % 2].dma_start(T.y[:, 256 * a + b0 * YB:256 * a + b1 * YB],
                                                T.ysb[32 * a:32 * a + 32, b0 * YB:b1 * YB]).then_inc(S.ys, 16)
    g.sync.wait_ge(S.ys, 128)
